import numpy as np
import ml_dtypes


def mxq(x, axis, fmt="e4m3"):
    dtype, down = {"e4m3": (ml_dtypes.float8_e4m3fn, 7), "e5m2": (ml_dtypes.float8_e5m2, 14)}[fmt]
    v = np.moveaxis(np.asarray(x, np.float32).astype(ml_dtypes.bfloat16).astype(np.float64), axis, -1)
    blocks = v.reshape(v.shape[:-1] + (-1, 32))
    amax = np.abs(blocks).max(-1, keepdims=True)
    byte = np.maximum(np.where(amax > 0, np.frexp(amax)[1] - 1 + 127, 0) - down, 1)
    scale = np.exp2(byte - 127.0)
    codes = (blocks / scale).astype(np.float32).astype(dtype).astype(np.float64)
    return np.moveaxis((codes * scale).reshape(v.shape), -1, axis)


WIDE = False


def mx_kscale(k):
    if not WIDE:
        return np.ones(k)
    levels = np.array([10, -10, 5, -5, 0])
    if k % 512:
        return np.exp2(np.random.permutation(np.resize(levels, k // 32))).repeat(32)
    a = np.empty((k // 512, 16))
    for p in range(k // 512):
        a[p, :8] = np.random.permutation(np.resize(levels, 8))
        for g in range(8):
            far = levels[np.abs(levels - a[p, g]) >= 10]
            a[p, g + 8] = far[np.random.randint(len(far))]
    return np.exp2(a.ravel()).repeat(32)


def f64(x):
    return np.asarray(x).astype(np.float64)


def striped(idx):
    return np.tile(idx.reshape(-1, 16).T, (8, 1)).astype(np.uint16)


def unstriped(offs):
    return offs[:16].T.reshape(-1).astype(np.int64)


def striped8(idx):
    return np.concatenate([x.reshape(-1, 16).T for x in idx]).astype(np.uint16)


def runs(offs, k):
    lists = np.stack([offs[16 * r : 16 * r + 16].T.reshape(-1) for r in range(8)]).astype(np.int64)
    return lists[np.arange(k) % 512 // 64]


def pack_weight(w):
    k, n = w.shape
    w = f64(np.asarray(w, np.float32).astype(ml_dtypes.bfloat16)).reshape(k // 32, 32, n)
    amax = np.abs(w).max(1)
    byte = np.clip(np.where(amax > 0, np.frexp(amax)[1] - 1 + 127 - 7, 1), 1, 254)
    scaled = (w * np.exp2(127.0 - byte)[:, None, :]).reshape(k, n).astype(np.float32)
    words = np.ascontiguousarray(scaled.reshape(k // 512, 128, 4, n).transpose(0, 1, 3, 2)).astype(ml_dtypes.float8_e4m3fn).view(np.uint8)
    return words, np.ascontiguousarray(byte.astype(np.uint8).reshape(k // 512, 16, n))


def unpack_weight(words, scales):
    g, p, n, _ = words.shape
    vals = np.ascontiguousarray(words).view(ml_dtypes.float8_e4m3fn).astype(np.float64) * np.repeat(np.exp2(scales.astype(np.float64) - 127.0), 8, axis=1)[..., None]
    return vals.transpose(0, 1, 3, 2).reshape(g * 512, n)


E2M1 = np.array([0.0, 0.5, 1.0, 1.5, 2.0, 3.0, 4.0, 6.0, -0.0, -0.5, -1.0, -1.5, -2.0, -3.0, -4.0, -6.0])


def pack_fp4(w):
    k, n = w.shape
    w = f64(np.asarray(w, np.float32).astype(ml_dtypes.bfloat16)).reshape(k // 32, 32, n)
    amax = np.abs(w).max(1)
    mant, ex = np.frexp(amax / 6.0)
    byte = np.clip(np.where(amax > 0, np.where(mant > 0.5, ex, ex - 1) + 127, 1), 1, 254)
    scaled = (w * np.exp2(127.0 - byte)[:, None, :]).reshape(k, n).astype(np.float32)
    c = np.ascontiguousarray(scaled.reshape(k // 512, 128, 4, n).transpose(0, 1, 3, 2)).astype(ml_dtypes.float4_e2m1fn).view(np.uint8) & 0xF
    words = (c[..., 0::2] | (c[..., 1::2] << 4)).reshape(k // 512, 128, 2 * n)
    return np.ascontiguousarray(words), np.ascontiguousarray(byte.astype(np.uint8).reshape(k // 512, 16, n))


def unpack_fp4(words, scales):
    g, _, n = scales.shape
    words = np.ascontiguousarray(words).reshape(g, 128, n, 2)
    nib = np.empty((g, 128, n, 4), np.uint8)
    nib[..., 0::2] = words & 0xF
    nib[..., 1::2] = words >> 4
    vals = E2M1[nib] * np.repeat(np.exp2(scales.astype(np.float64) - 127.0), 8, axis=1)[..., None]
    return vals.transpose(0, 1, 3, 2).reshape(g * 512, n)


K, T, S, H, G, W = 512, 1024, 256, 512, 2048, 128


def setup_inputs():
    n = np.random.standard_normal
    s = mx_kscale(K)[:, None]
    packed_xT = pack_weight(n((K, T)) * s)
    packed_w1 = pack_fp4(n((K, H)) / np.sqrt(K) / s)
    packed_dT = pack_weight(n((K, G)) / s)
    perm = np.random.permutation(S)
    return {
        "x_words": packed_xT[0],
        "x_scales": packed_xT[1],
        "w1_words": packed_w1[0],
        "w1_scales": packed_w1[1],
        "gs": (np.random.uniform(0.5, 1.5, (K, 1)) * s).astype(np.float32),
        "d_words": packed_dT[0],
        "d_scales": packed_dT[1],
        "offs": striped(np.random.permutation(T)[:S]),
        "k1": striped8(np.random.randint(0, G, (8, H))),
        "k2": striped8(np.random.randint(0, G, (8, H))),
        "two": striped(np.random.permutation(T)[:S]),
        "n1": striped(perm[:W]),
        "n2": striped(perm[W:]),
        "n3": striped(np.random.permutation(S)),
    }


def reference(x_words, x_scales, w1_words, w1_scales, gs, d_words, d_scales, offs, k1, k2, two, n1, n2, n3):
    d_k1 = unpack_weight(d_words, d_scales)[np.arange(K)[:, None], runs(k1, K)]
    xq = unpack_weight(x_words, x_scales)[:, unstriped(offs)]
    y = unpack_fp4(w1_words, w1_scales).T @ xq
    z = f64(gs) * y
    d_k2 = unpack_weight(d_words, d_scales)[np.arange(K)[:, None], runs(k2, K)]
    x_two = unpack_weight(x_words, x_scales)[:, unstriped(two)]
    h = 0.0625 * ((d_k1.T @ mxq(z, 0, "e4m3") + d_k2.T @ x_two))
    pa = h[:, unstriped(n1)]
    pb = h[:, unstriped(n2)]
    rb = pa - pb
    ds = np.zeros((H, S))
    ds[:, unstriped(n1)] = pb
    dt = ds.copy()
    dt[:, unstriped(n2)] = rb
    return np.maximum(dt, 0.5 * dt[:, unstriped(n3)])

@@ -1,0 +1,199 @@
+from contextlib import ExitStack
+
+import concourse.mybir as mybir
+
+K, T, S, H, G, W = 512, 1024, 256, 512, 2048, 128
+FLOPS = 3 * 2 * K * H * S
+
+F32 = mybir.dt.float32
+BF16 = mybir.dt.bfloat16
+I32 = mybir.dt.int32
+U32 = mybir.dt.uint32
+U16 = mybir.dt.uint16
+U8 = mybir.dt.uint8
+FP8X4 = mybir.dt.float8_e4m3fn_x4
+FP4X4 = mybir.dt.float4_e2m1fn_x4
+ALU = mybir.AluOpType
+COPY = mybir.ActivationFunctionType.Copy
+
+P = 128
+PACK = 4
+SPARE = 16
+HALF = 256
+
+
+def tile_picked_cmixiswapd_none_p_kernel(
+    tc, x_words, x_scales, w1_words, w1_scales, gs, d_words, d_scales, offs, k1, k2, two, n1, n2, n3, out
+):
+    nc = tc.nc
+    with ExitStack() as ctx:
+        keep = ctx.enter_context(tc.tile_pool(name="keep", bufs=1))
+        psum = ctx.enter_context(tc.psum_pool(name="psum", bufs=1))
+
+        def sb(name, shape, dtype):
+            return keep.tile(shape, dtype, name=name, align_bytes=64)
+
+        def load_list(name, src):
+            tile = sb(name, [P, src.shape[1]], U16)
+            nc.sync.dma_start(tile[:], src)
+            return tile
+
+        def load_plane(queues, tile, src):
+            for q in range(4):
+                queues[q].dma_start(tile[32 * q : 32 * q + 4, :].bitcast(I32), src[0, 4 * q : 4 * q + 4, :].bitcast(I32))
+
+        xw = sb("xw", [P, T], U32)
+        xs = sb("xs", [P, T], U8)
+        dw = sb("dw", [P, G], U32)
+        ds = sb("ds", [P, G], U8)
+        w1w = sb("w1w", [P, 2 * H], U8)
+        w1s = sb("w1s", [P, H], U8)
+        gain = sb("gain", [P, PACK], F32)
+        plane = sb("plane", [P, 2 * HALF], U8)
+
+        nc.vector.memset(xs[:].bitcast(I32), 0)
+        nc.vector.memset(w1s[:].bitcast(I32), 0)
+        nc.vector.memset(ds[:].bitcast(I32), 0)
+        nc.vector.memset(plane[:].bitcast(I32), 0)
+
+        windows = [sb("dt%d" % i, [P, S + SPARE], F32) for i in range(4)]
+        for window in windows:
+            nc.vector.memset(window[:, S:], 0.0)
+
+        l_offs = load_list("l_offs", offs)
+        nc.scalar.dma_start(w1w[:].bitcast(I32), w1_words[0].bitcast(I32))
+        l_two = load_list("l_two", two)
+        load_plane([nc.scalar, nc.scalar, nc.scalar, nc.sync], xs, x_scales)
+        nc.sync.dma_start(xw[:].bitcast(I32), x_words[0].rearrange("p n t -> p (n t)").bitcast(I32))
+        nc.gpsimd.dma_start(ds[0:P:8, :].bitcast(I32), d_scales[0].bitcast(I32))
+        nc.gpsimd.dma_start(gain[:], gs.rearrange("(p t) o -> p (t o)", t=PACK))
+        load_plane([nc.scalar] * 4, w1s, w1_scales)
+        l_k1 = load_list("l_k1", k1)
+        l_k2 = load_list("l_k2", k2)
+        nc.sync.dma_start(dw[:].bitcast(I32), d_words[0].rearrange("p n t -> p (n t)").bitcast(I32))
+        l_n1 = load_list("l_n1", n1)
+        l_n2 = load_list("l_n2", n2)
+        l_n3 = load_list("l_n3", n3)
+
+        xq_s = sb("xq_s", [P, S], U8)
+        xq_w = sb("xq_w", [P, S], U32)
+        xt_s = sb("xt_s", [P, S], U8)
+        xt_w = sb("xt_w", [P, S], U32)
+        nc.vector.tensor_copy(xq_s[:], xs[:].indirect(l_offs[:]))
+        nc.vector.tensor_copy(xt_s[:], xs[:].indirect(l_two[:]))
+        nc.vector.tensor_copy(xq_w[:], xw[:].indirect(l_offs[:]))
+        nc.vector.tensor_copy(xt_w[:], xw[:].indirect(l_two[:]))
+
+        w1w_d = sb("w1w_d", [P, 2 * H], U8)
+        w1s_d = sb("w1s_d", [P, H], U8)
+        nc.scalar.copy(
+            w1w_d[:].bitcast(U16).rearrange("p (t m) -> p t m", t=PACK),
+            w1w[:].bitcast(U16).rearrange("p (m t) -> p t m", t=PACK),
+        )
+        nc.gpsimd.tensor_copy(
+            w1s_d[:].rearrange("p (t m) -> p t m", t=PACK), w1s[:].rearrange("p (m t) -> p t m", t=PACK)
+        )
+
+        def first_product(dst, t, cols):
+            nc.tensor.matmul_mx(
+                out=dst,
+                lhsT=w1w_d[:, 2 * P * t : 2 * P * (t + 1)].bitcast(FP4X4),
+                lhsT_scale=w1s_d[:, P * t : P * (t + 1)],
+                rhs=xq_w[:, cols].bitcast(FP8X4),
+                rhs_scale=xq_s[:, cols],
+                start=True,
+                stop=True,
+            )
+
+        y_lo = [psum.tile([P, 2, P], F32, name="y_lo%d" % u) for u in range(2)]
+        y_hi = psum.tile([P, PACK, P], F32, name="y_hi")
+        for t in range(PACK):
+            first_product(y_lo[t // 2][:, t % 2, :], t, slice(0, P))
+        for t in range(PACK):
+            first_product(y_hi[:, t, :], t, slice(P, S))
+
+        picked_s = sb("picked_s", [P, 2 * HALF], U8)
+        dk1 = sb("dk1", [P, HALF], U32)
+        dk2 = sb("dk2", [P, HALF], U32)
+
+        def entries(lst, a):
+            return lst[:, a * HALF // 16 : (a + 1) * HALF // 16]
+
+        def pick_scales(a):
+            nc.vector.tensor_copy(picked_s[:, 0:HALF], ds[:].indirect(entries(l_k1, a)))
+            nc.vector.tensor_copy(picked_s[:, HALF : 2 * HALF], ds[:].indirect(entries(l_k2, a)))
+            for j in range(4):
+                nc.sync.dma_start(plane[j:P:32, :].bitcast(I32), picked_s[8 * j : P : 32, :].bitcast(I32))
+
+        pick_scales(0)
+
+        z = sb("z", [P, S, PACK], BF16)
+        for t in range(PACK):
+            nc.scalar.activation(z[:, 0:P, t], y_lo[t // 2][:, t % 2, :], COPY, scale=gain[:, t : t + 1])
+        nc.vector.tensor_tensor(
+            z[:, P:S, :],
+            y_hi[:].rearrange("p t n -> p n t"),
+            gain[:].unsqueeze(1).to_broadcast([P, P, PACK]),
+            ALU.mult,
+        )
+        nc.vector.tensor_copy(dk2[:], dw[:].indirect(entries(l_k2, 0)))
+        zq_w = sb("zq_w", [P, S], U32)
+        zq_s = sb("zq_s", [P, S], U8)
+        nc.vector.quantize_mx(out=zq_w[:].bitcast(FP8X4), scales=zq_s[:], in_=z[:].rearrange("p n t -> p (n t)"))
+        nc.vector.tensor_copy(dk1[:], dw[:].indirect(entries(l_k1, 0)))
+
+        def second_product(i):
+            c = i % 2
+            acc = psum.tile([P, S], F32, name="acc%d" % i)
+            nc.tensor.matmul_mx(
+                out=acc[:],
+                lhsT=dk2[:, P * c : P * (c + 1)].bitcast(FP8X4),
+                lhsT_scale=plane[:, HALF + P * c : HALF + P * (c + 1)],
+                rhs=xt_w[:].bitcast(FP8X4),
+                rhs_scale=xt_s[:],
+                start=True,
+                stop=False,
+            )
+            nc.tensor.matmul_mx(
+                out=acc[:],
+                lhsT=dk1[:, P * c : P * (c + 1)].bitcast(FP8X4),
+                lhsT_scale=plane[:, P * c : P * (c + 1)],
+                rhs=zq_w[:].bitcast(FP8X4),
+                rhs_scale=zq_s[:],
+                start=False,
+                stop=True,
+            )
+            h = sb("h%d" % i, [P, S], F32)
+            if i == 0:
+                nc.scalar.activation(h[:], acc[:], COPY, scale=0.0625)
+            else:
+                nc.vector.tensor_scalar(h[:], acc[:], 0.0625, None, ALU.mult)
+            return h
+
+        def swap_columns(tiles, hs):
+            pa = {i: sb("pa%d" % i, [P, W], F32) for i in tiles}
+            pb = {i: sb("pb%d" % i, [P, W], F32) for i in tiles}
+            rb = {i: sb("rb%d" % i, [P, W], F32) for i in tiles}
+            dt = windows
+            far = {i: sb("far%d" % i, [P, S], F32) for i in tiles}
+            res = {i: sb("res%d" % i, [P, S], F32) for i in tiles}
+            for i in tiles:
+                nc.scalar.activation(pb[i][:], hs[i][:].indirect(l_n2[:]), COPY)
+                nc.scalar.activation(pa[i][:], hs[i][:].indirect(l_n1[:]), COPY)
+                nc.vector.tensor_tensor(rb[i][:], pa[i][:], pb[i][:], ALU.subtract)
+            for i in tiles:
+                nc.scalar.activation(dt[i][:].indirect(l_n1[:]), pb[i][:], COPY)
+            for i in tiles:
+                nc.scalar.activation(dt[i][:].indirect(l_n2[:]), rb[i][:], COPY)
+            for i in tiles:
+                nc.scalar.activation(far[i][:], dt[i][:].indirect(l_n3[:]), COPY)
+                nc.vector.scalar_tensor_tensor(res[i][:], far[i][:], 0.5, dt[i][:, 0:S], ALU.mult, ALU.max)
+                nc.sync.dma_start(out[P * i : P * (i + 1), :], res[i][:])
+
+        hs = {i: second_product(i) for i in (0, 1)}
+        pick_scales(1)
+        nc.vector.tensor_copy(dk2[:], dw[:].indirect(entries(l_k2, 1)))
+        nc.vector.tensor_copy(dk1[:], dw[:].indirect(entries(l_k1, 1)))
+        swap_columns((0, 1), hs)
+        hs = {i: second_product(i) for i in (2, 3)}
+        swap_columns((2, 3), hs)

@@ -18,6 +18,8 @@ COPY = mybir.ActivationFunctionType.Copy
 
 P = 128
 PACK = 4
+D_SYNC = 1536
+LAST = 64
 SPARE = 16
 HALF = 256
 
@@ -30,17 +32,17 @@ def tile_picked_cmixiswapd_none_p_kernel(
         keep = ctx.enter_context(tc.tile_pool(name="keep", bufs=1))
         psum = ctx.enter_context(tc.psum_pool(name="psum", bufs=1))
 
-        def sb(name, shape, dtype):
-            return keep.tile(shape, dtype, name=name, align_bytes=64)
+        def sb(name, shape, dtype, tag=None):
+            return keep.tile(shape, dtype, name=name, tag=tag or name, align_bytes=64)
 
         def load_list(name, src):
             tile = sb(name, [P, src.shape[1]], U16)
             nc.sync.dma_start(tile[:], src)
             return tile
 
-        def load_plane(queues, tile, src):
-            for q in range(4):
-                queues[q].dma_start(tile[32 * q : 32 * q + 4, :].bitcast(I32), src[0, 4 * q : 4 * q + 4, :].bitcast(I32))
+        def load_plane(tile, src, quadrants):
+            for q in quadrants:
+                nc.sync.dma_start(tile[32 * q : 32 * q + 4, :].bitcast(I32), src[0, 4 * q : 4 * q + 4, :].bitcast(I32))
 
         xw = sb("xw", [P, T], U32)
         xs = sb("xs", [P, T], U8)
@@ -51,38 +53,36 @@ def tile_picked_cmixiswapd_none_p_kernel(
         gain = sb("gain", [P, PACK], F32)
         plane = sb("plane", [P, 2 * HALF], U8)
 
-        nc.vector.memset(xs[:].bitcast(I32), 0)
-        nc.vector.memset(w1s[:].bitcast(I32), 0)
+        nc.gpsimd.memset(xs[:].bitcast(I32), 0)
         nc.vector.memset(ds[:].bitcast(I32), 0)
+        nc.vector.memset(w1s[:].bitcast(I32), 0)
         nc.vector.memset(plane[:].bitcast(I32), 0)
 
         windows = [sb("dt%d" % i, [P, S + SPARE], F32) for i in range(4)]
         for window in windows:
             nc.vector.memset(window[:, S:], 0.0)
 
-        l_offs = load_list("l_offs", offs)
-        nc.scalar.dma_start(w1w[:].bitcast(I32), w1_words[0].bitcast(I32))
-        l_two = load_list("l_two", two)
-        load_plane([nc.scalar, nc.scalar, nc.scalar, nc.sync], xs, x_scales)
-        nc.sync.dma_start(xw[:].bitcast(I32), x_words[0].rearrange("p n t -> p (n t)").bitcast(I32))
-        nc.gpsimd.dma_start(ds[0:P:8, :].bitcast(I32), d_scales[0].bitcast(I32))
-        nc.gpsimd.dma_start(gain[:], gs.rearrange("(p t) o -> p (t o)", t=PACK))
-        load_plane([nc.scalar] * 4, w1s, w1_scales)
         l_k1 = load_list("l_k1", k1)
         l_k2 = load_list("l_k2", k2)
-        nc.sync.dma_start(dw[:].bitcast(I32), d_words[0].rearrange("p n t -> p (n t)").bitcast(I32))
-        l_n1 = load_list("l_n1", n1)
-        l_n2 = load_list("l_n2", n2)
-        l_n3 = load_list("l_n3", n3)
+        l_offs = load_list("l_offs", offs)
+        nc.sync.dma_start(ds[0:P:8, :].bitcast(I32), d_scales[0].bitcast(I32))
+        load_plane(xs, x_scales, range(3))
+        nc.sync.dma_start(xw[:].bitcast(I32), x_words[0].rearrange("p n t -> p (n t)").bitcast(I32))
+        nc.gpsimd.dma_start(w1w[:].bitcast(I32), w1_words[0].bitcast(I32))
+        d_i32 = d_words[0].rearrange("p n t -> p (n t)").bitcast(I32)
+        nc.gpsimd.dma_start(dw[:, D_SYNC:G].bitcast(I32), d_i32[:, D_SYNC:G])
+        nc.gpsimd.dma_start(gain[:], gs.rearrange("(p t) o -> p (t o)", t=PACK))
+        load_plane(xs, x_scales, range(3, 4))
+        l_two = load_list("l_two", two)
+        load_plane(w1s, w1_scales, range(4))
+        nc.sync.dma_start(dw[:, 0:D_SYNC].bitcast(I32), d_i32[:, 0:D_SYNC])
 
         xq_s = sb("xq_s", [P, S], U8)
         xq_w = sb("xq_w", [P, S], U32)
         xt_s = sb("xt_s", [P, S], U8)
         xt_w = sb("xt_w", [P, S], U32)
         nc.vector.tensor_copy(xq_s[:], xs[:].indirect(l_offs[:]))
-        nc.vector.tensor_copy(xt_s[:], xs[:].indirect(l_two[:]))
         nc.vector.tensor_copy(xq_w[:], xw[:].indirect(l_offs[:]))
-        nc.vector.tensor_copy(xt_w[:], xw[:].indirect(l_two[:]))
 
         w1w_d = sb("w1w_d", [P, 2 * H], U8)
         w1s_d = sb("w1s_d", [P, H], U8)
@@ -108,24 +108,28 @@ def tile_picked_cmixiswapd_none_p_kernel(
         y_lo = [psum.tile([P, 2, P], F32, name="y_lo%d" % u) for u in range(2)]
         y_hi = psum.tile([P, PACK, P], F32, name="y_hi")
         for t in range(PACK):
-            first_product(y_lo[t // 2][:, t % 2, :], t, slice(0, P))
-        for t in range(PACK):
             first_product(y_hi[:, t, :], t, slice(P, S))
+        for t in range(PACK):
+            first_product(y_lo[t // 2][:, t % 2, :], t, slice(0, P))
 
-        picked_s = sb("picked_s", [P, 2 * HALF], U8)
-        dk1 = sb("dk1", [P, HALF], U32)
-        dk2 = sb("dk2", [P, HALF], U32)
+        dk1 = [sb("dk1_0", [P, HALF], U32)]
+        dk2 = [sb("dk2_0", [P, HALF], U32)]
 
         def entries(lst, a):
             return lst[:, a * HALF // 16 : (a + 1) * HALF // 16]
 
-        def pick_scales(a):
+        def pick_scales(a, picked_s):
             nc.vector.tensor_copy(picked_s[:, 0:HALF], ds[:].indirect(entries(l_k1, a)))
             nc.vector.tensor_copy(picked_s[:, HALF : 2 * HALF], ds[:].indirect(entries(l_k2, a)))
             for j in range(4):
                 nc.sync.dma_start(plane[j:P:32, :].bitcast(I32), picked_s[8 * j : P : 32, :].bitcast(I32))
 
-        pick_scales(0)
+        pick_scales(0, sb("picked_s0", [P, 2 * HALF], U8))
+        l_n1 = load_list("l_n1", n1)
+        l_n2 = load_list("l_n2", n2)
+        l_n3 = load_list("l_n3", n3)
+        nc.vector.tensor_copy(xt_s[:], xs[:].indirect(l_two[:]))
+        nc.vector.tensor_copy(xt_w[:], xw[:].indirect(l_two[:]))
 
         z = sb("z", [P, S, PACK], BF16)
         for t in range(PACK):
@@ -136,18 +140,18 @@ def tile_picked_cmixiswapd_none_p_kernel(
             gain[:].unsqueeze(1).to_broadcast([P, P, PACK]),
             ALU.mult,
         )
-        nc.vector.tensor_copy(dk2[:], dw[:].indirect(entries(l_k2, 0)))
+        nc.vector.tensor_copy(dk2[0][:], dw[:].indirect(entries(l_k2, 0)))
         zq_w = sb("zq_w", [P, S], U32)
         zq_s = sb("zq_s", [P, S], U8)
         nc.vector.quantize_mx(out=zq_w[:].bitcast(FP8X4), scales=zq_s[:], in_=z[:].rearrange("p n t -> p (n t)"))
-        nc.vector.tensor_copy(dk1[:], dw[:].indirect(entries(l_k1, 0)))
+        nc.vector.tensor_copy(dk1[0][:], dw[:].indirect(entries(l_k1, 0)))
 
         def second_product(i):
-            c = i % 2
+            a, c = divmod(i, 2)
             acc = psum.tile([P, S], F32, name="acc%d" % i)
             nc.tensor.matmul_mx(
                 out=acc[:],
-                lhsT=dk2[:, P * c : P * (c + 1)].bitcast(FP8X4),
+                lhsT=dk2[a][:, P * c : P * (c + 1)].bitcast(FP8X4),
                 lhsT_scale=plane[:, HALF + P * c : HALF + P * (c + 1)],
                 rhs=xt_w[:].bitcast(FP8X4),
                 rhs_scale=xt_s[:],
@@ -156,7 +160,7 @@ def tile_picked_cmixiswapd_none_p_kernel(
             )
             nc.tensor.matmul_mx(
                 out=acc[:],
-                lhsT=dk1[:, P * c : P * (c + 1)].bitcast(FP8X4),
+                lhsT=dk1[a][:, P * c : P * (c + 1)].bitcast(FP8X4),
                 lhsT_scale=plane[:, P * c : P * (c + 1)],
                 rhs=zq_w[:].bitcast(FP8X4),
                 rhs_scale=zq_s[:],
@@ -186,14 +190,20 @@ def tile_picked_cmixiswapd_none_p_kernel(
             for i in tiles:
                 nc.scalar.activation(dt[i][:].indirect(l_n2[:]), rb[i][:], COPY)
             for i in tiles:
-                nc.scalar.activation(far[i][:], dt[i][:].indirect(l_n3[:]), COPY)
-                nc.vector.scalar_tensor_tensor(res[i][:], far[i][:], 0.5, dt[i][:, 0:S], ALU.mult, ALU.max)
-                nc.sync.dma_start(out[P * i : P * (i + 1), :], res[i][:])
+                cuts = (0, S - LAST, S) if i == 3 else (0, S)
+                for lo, hi in zip(cuts, cuts[1:]):
+                    nc.scalar.activation(far[i][:, lo:hi], dt[i][:].indirect(l_n3[:, lo // 16 : hi // 16]), COPY)
+                    nc.vector.scalar_tensor_tensor(
+                        res[i][:, lo:hi], far[i][:, lo:hi], 0.5, dt[i][:, lo:hi], ALU.mult, ALU.max
+                    )
+                    nc.sync.dma_start(out[P * i : P * (i + 1), lo:hi], res[i][:, lo:hi])
 
         hs = {i: second_product(i) for i in (0, 1)}
-        pick_scales(1)
-        nc.vector.tensor_copy(dk2[:], dw[:].indirect(entries(l_k2, 1)))
-        nc.vector.tensor_copy(dk1[:], dw[:].indirect(entries(l_k1, 1)))
+        pick_scales(1, sb("picked_s1", [P, 2 * HALF], U8, tag="z"))
         swap_columns((0, 1), hs)
+        dk2.append(sb("dk2_1", [P, HALF], U32, tag="pa0"))
+        dk1.append(sb("dk1_1", [P, HALF], U32, tag="pa1"))
+        nc.vector.tensor_copy(dk2[1][:], dw[:].indirect(entries(l_k2, 1)))
+        nc.vector.tensor_copy(dk1[1][:], dw[:].indirect(entries(l_k1, 1)))
         hs = {i: second_product(i) for i in (2, 3)}
         swap_columns((2, 3), hs)

@@ -18,7 +18,6 @@ COPY = mybir.ActivationFunctionType.Copy
 
 P = 128
 PACK = 4
-D_SYNC = 1536
 LAST = 64
 SPARE = 16
 HALF = 256
@@ -40,8 +39,8 @@ def tile_picked_cmixiswapd_none_p_kernel(
             nc.sync.dma_start(tile[:], src)
             return tile
 
-        def load_plane(tile, src, quadrants):
-            for q in quadrants:
+        def load_plane(tile, src):
+            for q in range(4):
                 nc.sync.dma_start(tile[32 * q : 32 * q + 4, :].bitcast(I32), src[0, 4 * q : 4 * q + 4, :].bitcast(I32))
 
         xw = sb("xw", [P, T], U32)
@@ -53,9 +52,9 @@ def tile_picked_cmixiswapd_none_p_kernel(
         gain = sb("gain", [P, PACK], F32)
         plane = sb("plane", [P, 2 * HALF], U8)
 
-        nc.gpsimd.memset(xs[:].bitcast(I32), 0)
-        nc.vector.memset(ds[:].bitcast(I32), 0)
         nc.vector.memset(w1s[:].bitcast(I32), 0)
+        nc.vector.memset(ds[:].bitcast(I32), 0)
+        nc.vector.memset(xs[:].bitcast(I32), 0)
         nc.vector.memset(plane[:].bitcast(I32), 0)
 
         windows = [sb("dt%d" % i, [P, S + SPARE], F32) for i in range(4)]
@@ -64,18 +63,15 @@ def tile_picked_cmixiswapd_none_p_kernel(
 
         l_k1 = load_list("l_k1", k1)
         l_k2 = load_list("l_k2", k2)
-        l_offs = load_list("l_offs", offs)
+        load_plane(w1s, w1_scales)
         nc.sync.dma_start(ds[0:P:8, :].bitcast(I32), d_scales[0].bitcast(I32))
-        load_plane(xs, x_scales, range(3))
         nc.sync.dma_start(xw[:].bitcast(I32), x_words[0].rearrange("p n t -> p (n t)").bitcast(I32))
         nc.gpsimd.dma_start(w1w[:].bitcast(I32), w1_words[0].bitcast(I32))
-        d_i32 = d_words[0].rearrange("p n t -> p (n t)").bitcast(I32)
-        nc.gpsimd.dma_start(dw[:, D_SYNC:G].bitcast(I32), d_i32[:, D_SYNC:G])
         nc.gpsimd.dma_start(gain[:], gs.rearrange("(p t) o -> p (t o)", t=PACK))
-        load_plane(xs, x_scales, range(3, 4))
+        l_offs = load_list("l_offs", offs)
+        load_plane(xs, x_scales)
         l_two = load_list("l_two", two)
-        load_plane(w1s, w1_scales, range(4))
-        nc.sync.dma_start(dw[:, 0:D_SYNC].bitcast(I32), d_i32[:, 0:D_SYNC])
+        nc.sync.dma_start(dw[:].bitcast(I32), d_words[0].rearrange("p n t -> p (n t)").bitcast(I32))
 
         xq_s = sb("xq_s", [P, S], U8)
         xq_w = sb("xq_w", [P, S], U32)
@@ -90,7 +86,7 @@ def tile_picked_cmixiswapd_none_p_kernel(
             w1w_d[:].bitcast(U16).rearrange("p (t m) -> p t m", t=PACK),
             w1w[:].bitcast(U16).rearrange("p (m t) -> p t m", t=PACK),
         )
-        nc.gpsimd.tensor_copy(
+        nc.vector.tensor_copy(
             w1s_d[:].rearrange("p (t m) -> p t m", t=PACK), w1s[:].rearrange("p (m t) -> p t m", t=PACK)
         )
 
@@ -107,10 +103,12 @@ def tile_picked_cmixiswapd_none_p_kernel(
 
         y_lo = [psum.tile([P, 2, P], F32, name="y_lo%d" % u) for u in range(2)]
         y_hi = psum.tile([P, PACK, P], F32, name="y_hi")
+        for t in (0, 1):
+            first_product(y_lo[0][:, t, :], t, slice(0, P))
         for t in range(PACK):
             first_product(y_hi[:, t, :], t, slice(P, S))
-        for t in range(PACK):
-            first_product(y_lo[t // 2][:, t % 2, :], t, slice(0, P))
+        for t in (2, 3):
+            first_product(y_lo[1][:, t - 2, :], t, slice(0, P))
 
         dk1 = [sb("dk1_0", [P, HALF], U32)]
         dk2 = [sb("dk2_0", [P, HALF], U32)]

@@ -66,10 +66,10 @@ def tile_picked_cmixiswapd_none_p_kernel(
         load_plane(w1s, w1_scales)
         nc.sync.dma_start(ds[0:P:8, :].bitcast(I32), d_scales[0].bitcast(I32))
         nc.sync.dma_start(xw[:].bitcast(I32), x_words[0].rearrange("p n t -> p (n t)").bitcast(I32))
-        nc.gpsimd.dma_start(w1w[:].bitcast(I32), w1_words[0].bitcast(I32))
         nc.gpsimd.dma_start(gain[:], gs.rearrange("(p t) o -> p (t o)", t=PACK))
         l_offs = load_list("l_offs", offs)
         load_plane(xs, x_scales)
+        nc.sync.dma_start(w1w[:].bitcast(I32), w1_words[0].bitcast(I32))
         l_two = load_list("l_two", two)
         nc.sync.dma_start(dw[:].bitcast(I32), d_words[0].rearrange("p n t -> p (n t)").bitcast(I32))
 
@@ -86,7 +86,7 @@ def tile_picked_cmixiswapd_none_p_kernel(
             w1w_d[:].bitcast(U16).rearrange("p (t m) -> p t m", t=PACK),
             w1w[:].bitcast(U16).rearrange("p (m t) -> p t m", t=PACK),
         )
-        nc.vector.tensor_copy(
+        nc.gpsimd.tensor_copy(
             w1s_d[:].rearrange("p (t m) -> p t m", t=PACK), w1s[:].rearrange("p (m t) -> p t m", t=PACK)
         )
 
@@ -197,7 +197,7 @@ def tile_picked_cmixiswapd_none_p_kernel(
                     nc.sync.dma_start(out[P * i : P * (i + 1), lo:hi], res[i][:, lo:hi])
 
         hs = {i: second_product(i) for i in (0, 1)}
-        pick_scales(1, sb("picked_s1", [P, 2 * HALF], U8, tag="z"))
+        pick_scales(1, sb("picked_s1", [P, 2 * HALF], U8, tag="dk1_0"))
         swap_columns((0, 1), hs)
         dk2.append(sb("dk2_1", [P, HALF], U32, tag="pa0"))
         dk1.append(sb("dk1_1", [P, HALF], U32, tag="pa1"))

from contextlib import ExitStack

import concourse.mybir as mybir

K, T, S, H, G, W = 512, 1024, 256, 512, 2048, 128
FLOPS = 3 * 2 * K * H * S

F32 = mybir.dt.float32
BF16 = mybir.dt.bfloat16
I32 = mybir.dt.int32
U32 = mybir.dt.uint32
U16 = mybir.dt.uint16
U8 = mybir.dt.uint8
FP8X4 = mybir.dt.float8_e4m3fn_x4
FP4X4 = mybir.dt.float4_e2m1fn_x4
ALU = mybir.AluOpType
COPY = mybir.ActivationFunctionType.Copy

P = 128
PACK = 4
LAST = 64
SPARE = 16
HALF = 256


def tile_picked_cmixiswapd_none_p_kernel(
    tc, x_words, x_scales, w1_words, w1_scales, gs, d_words, d_scales, offs, k1, k2, two, n1, n2, n3, out
):
    nc = tc.nc
    with ExitStack() as ctx:
        keep = ctx.enter_context(tc.tile_pool(name="keep", bufs=1))
        psum = ctx.enter_context(tc.psum_pool(name="psum", bufs=1))

        def sb(name, shape, dtype, tag=None):
            return keep.tile(shape, dtype, name=name, tag=tag or name, align_bytes=64)

        def load_list(name, src):
            tile = sb(name, [P, src.shape[1]], U16)
            nc.sync.dma_start(tile[:], src)
            return tile

        def load_plane(tile, src):
            for q in range(4):
                nc.sync.dma_start(tile[32 * q : 32 * q + 4, :].bitcast(I32), src[0, 4 * q : 4 * q + 4, :].bitcast(I32))

        xw = sb("xw", [P, T], U32)
        xs = sb("xs", [P, T], U8)
        dw = sb("dw", [P, G], U32)
        ds = sb("ds", [P, G], U8)
        w1w = sb("w1w", [P, 2 * H], U8)
        w1s = sb("w1s", [P, H], U8)
        gain = sb("gain", [P, PACK], F32)
        plane = sb("plane", [P, 2 * HALF], U8)

        nc.vector.memset(w1s[:].bitcast(I32), 0)
        nc.vector.memset(ds[:].bitcast(I32), 0)
        nc.vector.memset(xs[:].bitcast(I32), 0)
        nc.vector.memset(plane[:].bitcast(I32), 0)

        windows = [sb("dt%d" % i, [P, S + SPARE], F32) for i in range(4)]
        for window in windows:
            nc.vector.memset(window[:, S:], 0.0)

        l_k1 = load_list("l_k1", k1)
        l_k2 = load_list("l_k2", k2)
        load_plane(w1s, w1_scales)
        nc.sync.dma_start(ds[0:P:8, :].bitcast(I32), d_scales[0].bitcast(I32))
        nc.sync.dma_start(xw[:].bitcast(I32), x_words[0].rearrange("p n t -> p (n t)").bitcast(I32))
        nc.gpsimd.dma_start(gain[:], gs.rearrange("(p t) o -> p (t o)", t=PACK))
        l_offs = load_list("l_offs", offs)
        load_plane(xs, x_scales)
        nc.sync.dma_start(w1w[:].bitcast(I32), w1_words[0].bitcast(I32))
        l_two = load_list("l_two", two)
        nc.sync.dma_start(dw[:].bitcast(I32), d_words[0].rearrange("p n t -> p (n t)").bitcast(I32))

        xq_s = sb("xq_s", [P, S], U8)
        xq_w = sb("xq_w", [P, S], U32)
        xt_s = sb("xt_s", [P, S], U8)
        xt_w = sb("xt_w", [P, S], U32)
        nc.vector.tensor_copy(xq_s[:], xs[:].indirect(l_offs[:]))
        nc.vector.tensor_copy(xq_w[:], xw[:].indirect(l_offs[:]))

        w1w_d = sb("w1w_d", [P, 2 * H], U8)
        w1s_d = sb("w1s_d", [P, H], U8)
        nc.scalar.copy(
            w1w_d[:].bitcast(U16).rearrange("p (t m) -> p t m", t=PACK),
            w1w[:].bitcast(U16).rearrange("p (m t) -> p t m", t=PACK),
        )
        nc.gpsimd.tensor_copy(
            w1s_d[:].rearrange("p (t m) -> p t m", t=PACK), w1s[:].rearrange("p (m t) -> p t m", t=PACK)
        )

        def first_product(dst, t, cols):
            nc.tensor.matmul_mx(
                out=dst,
                lhsT=w1w_d[:, 2 * P * t : 2 * P * (t + 1)].bitcast(FP4X4),
                lhsT_scale=w1s_d[:, P * t : P * (t + 1)],
                rhs=xq_w[:, cols].bitcast(FP8X4),
                rhs_scale=xq_s[:, cols],
                start=True,
                stop=True,
            )

        y_lo = [psum.tile([P, 2, P], F32, name="y_lo%d" % u) for u in range(2)]
        y_hi = psum.tile([P, PACK, P], F32, name="y_hi")
        for t in (0, 1):
            first_product(y_lo[0][:, t, :], t, slice(0, P))
        for t in range(PACK):
            first_product(y_hi[:, t, :], t, slice(P, S))
        for t in (2, 3):
            first_product(y_lo[1][:, t - 2, :], t, slice(0, P))

        dk1 = [sb("dk1_0", [P, HALF], U32)]
        dk2 = [sb("dk2_0", [P, HALF], U32)]

        def entries(lst, a):
            return lst[:, a * HALF // 16 : (a + 1) * HALF // 16]

        def pick_scales(a, picked_s):
            nc.vector.tensor_copy(picked_s[:, 0:HALF], ds[:].indirect(entries(l_k1, a)))
            nc.vector.tensor_copy(picked_s[:, HALF : 2 * HALF], ds[:].indirect(entries(l_k2, a)))
            for j in range(4):
                nc.sync.dma_start(plane[j:P:32, :].bitcast(I32), picked_s[8 * j : P : 32, :].bitcast(I32))

        pick_scales(0, sb("picked_s0", [P, 2 * HALF], U8))
        l_n1 = load_list("l_n1", n1)
        l_n2 = load_list("l_n2", n2)
        l_n3 = load_list("l_n3", n3)
        nc.vector.tensor_copy(xt_s[:], xs[:].indirect(l_two[:]))
        nc.vector.tensor_copy(xt_w[:], xw[:].indirect(l_two[:]))

        z = sb("z", [P, S, PACK], BF16)
        for t in range(PACK):
            nc.scalar.activation(z[:, 0:P, t], y_lo[t // 2][:, t % 2, :], COPY, scale=gain[:, t : t + 1])
        nc.vector.tensor_tensor(
            z[:, P:S, :],
            y_hi[:].rearrange("p t n -> p n t"),
            gain[:].unsqueeze(1).to_broadcast([P, P, PACK]),
            ALU.mult,
        )
        nc.vector.tensor_copy(dk2[0][:], dw[:].indirect(entries(l_k2, 0)))
        zq_w = sb("zq_w", [P, S], U32)
        zq_s = sb("zq_s", [P, S], U8)
        nc.vector.quantize_mx(out=zq_w[:].bitcast(FP8X4), scales=zq_s[:], in_=z[:].rearrange("p n t -> p (n t)"))
        nc.vector.tensor_copy(dk1[0][:], dw[:].indirect(entries(l_k1, 0)))

        def second_product(i):
            a, c = divmod(i, 2)
            acc = psum.tile([P, S], F32, name="acc%d" % i)
            nc.tensor.matmul_mx(
                out=acc[:],
                lhsT=dk2[a][:, P * c : P * (c + 1)].bitcast(FP8X4),
                lhsT_scale=plane[:, HALF + P * c : HALF + P * (c + 1)],
                rhs=xt_w[:].bitcast(FP8X4),
                rhs_scale=xt_s[:],
                start=True,
                stop=False,
            )
            nc.tensor.matmul_mx(
                out=acc[:],
                lhsT=dk1[a][:, P * c : P * (c + 1)].bitcast(FP8X4),
                lhsT_scale=plane[:, P * c : P * (c + 1)],
                rhs=zq_w[:].bitcast(FP8X4),
                rhs_scale=zq_s[:],
                start=False,
                stop=True,
            )
            h = sb("h%d" % i, [P, S], F32)
            if i == 0:
                nc.scalar.activation(h[:], acc[:], COPY, scale=0.0625)
            else:
                nc.vector.tensor_scalar(h[:], acc[:], 0.0625, None, ALU.mult)
            return h

        def swap_columns(tiles, hs):
            pa = {i: sb("pa%d" % i, [P, W], F32) for i in tiles}
            pb = {i: sb("pb%d" % i, [P, W], F32) for i in tiles}
            rb = {i: sb("rb%d" % i, [P, W], F32) for i in tiles}
            dt = windows
            far = {i: sb("far%d" % i, [P, S], F32) for i in tiles}
            res = {i: sb("res%d" % i, [P, S], F32) for i in tiles}
            for i in tiles:
                nc.scalar.activation(pb[i][:], hs[i][:].indirect(l_n2[:]), COPY)
                nc.scalar.activation(pa[i][:], hs[i][:].indirect(l_n1[:]), COPY)
                nc.vector.tensor_tensor(rb[i][:], pa[i][:], pb[i][:], ALU.subtract)
            for i in tiles:
                nc.scalar.activation(dt[i][:].indirect(l_n1[:]), pb[i][:], COPY)
            for i in tiles:
                nc.scalar.activation(dt[i][:].indirect(l_n2[:]), rb[i][:], COPY)
            for i in tiles:
                cuts = (0, S - LAST, S) if i == 3 else (0, S)
                for lo, hi in zip(cuts, cuts[1:]):
                    nc.scalar.activation(far[i][:, lo:hi], dt[i][:].indirect(l_n3[:, lo // 16 : hi // 16]), COPY)
                    nc.vector.scalar_tensor_tensor(
                        res[i][:, lo:hi], far[i][:, lo:hi], 0.5, dt[i][:, lo:hi], ALU.mult, ALU.max
                    )
                    nc.sync.dma_start(out[P * i : P * (i + 1), lo:hi], res[i][:, lo:hi])

        hs = {i: second_product(i) for i in (0, 1)}
        pick_scales(1, sb("picked_s1", [P, 2 * HALF], U8, tag="dk1_0"))
        swap_columns((0, 1), hs)
        dk2.append(sb("dk2_1", [P, HALF], U32, tag="pa0"))
        dk1.append(sb("dk1_1", [P, HALF], U32, tag="pa1"))
        nc.vector.tensor_copy(dk2[1][:], dw[:].indirect(entries(l_k2, 1)))
        nc.vector.tensor_copy(dk1[1][:], dw[:].indirect(entries(l_k1, 1)))
        hs = {i: second_product(i) for i in (2, 3)}
        swap_columns((2, 3), hs)
